import numpy as np, ml_dtypes
CORES = [25,29,65,69,153,157,193,197]
N = 8
BF = ml_dtypes.bfloat16
H, W, V, K, F, S, R, CAP = 2624, 2816, 512, 256, 2, 2, 3, 64
def start(q, ans):
    s = np.add.reduce(np.arange(1, 17)[:, None] * q, axis=-2) + ans
    return F * np.arange(K) + (s & (F - 1))
def parts(rng):
    return (rng.integers(0, 256, (N, 8, 16, H)), rng.integers(0, 256, (N, 8, 16, K)), rng.integers(0, H, (N, 8, 16, V)),
            np.ascontiguousarray(np.argsort(rng.random((N, 8, V)), axis=-1)), rng.integers(800, 961, (N, 8)))
def pack(x, q, p, mo, th):
    return {"x": np.ascontiguousarray(x).reshape(N, 128, H).astype(np.float32).astype(BF), "qs": np.ascontiguousarray(q).reshape(N, 128, K).astype(np.float32).astype(BF),
            "towns": np.ascontiguousarray(p).reshape(N, 128, V).astype(np.int32), "mo": np.ascontiguousarray(mo).astype(np.int32),
            "th": np.repeat(th, 16, axis=1).reshape(N, 128, 1).astype(np.int32)}
def mothers(rng, src, dst):
    m = np.zeros(V, np.int64); i = np.arange(V)
    m[src] = dst; m[np.setdiff1d(i, src)] = rng.permutation(np.setdiff1d(i, dst))
    return m
def setup_inputs(rng):
    return pack(*parts(rng))
def setup_inputs_room(rng):
    x, q, p, mo, th = parts(rng)
    x = rng.integers(0, 112, x.shape); th = rng.integers(1, 17, (N, 8))
    for a in range(N):
        for g in range(8):
            n = int(rng.choice(np.array([0, 1, CAP - 1, CAP, CAP + 1, K])))
            if a == 0: n = (CAP, CAP + 1, CAP - 1, 0, 1, K, CAP, K - 1)[g]
            hard = np.zeros(K, bool); hard[rng.permutation(K)[:n]] = True
            rec = rng.integers(0, H - K, K)
            w = np.where(hard, rng.integers(128, 256, (16, K)), x[a, g][:, rec]); w[0, hard] = 128 + 16 * a
            q[a, g] = w; u = start(w, 0)
            e = np.flatnonzero(~hard); p[a, g][rng.integers(0, 8, len(e)), u[e]] = rec[e]
            v = u
            for s in range(S): v = mo[a, g][v]
            b = np.flatnonzero(hard); b = b[rng.random(len(b)) < 0.5]; o = (a + 1) % N
            x[o, g][:, H - K + b] = w[:, b]; p[o, g][rng.integers(8, 16, len(b)), v[b]] = H - K + b
    return pack(x, q, p, mo, th)
def setup_inputs_ties(rng):
    x, q, p, mo, th = parts(rng); o = rng.permutation(8); i, e = o[:4], o[4:]
    x[:, i] = 64 * rng.integers(0, 4, (N, 4, 16, H)); q[:, i] = 64 * rng.integers(0, 4, (N, 4, 16, K))
    y = p[:, i]; y[:, :, 8:, 1::3] = y[:, :, :8, 1::3]; p[:, i] = y
    th[:, i] = rng.choice(np.array([768, 769, 832, 833, 896]), (N, 4))
    k = rng.integers(0, 3, (N, 4, 1, H)); y = np.where(k == 0, 0, np.where(k == 1, 255, x[:, e])); y[..., 0] = 255; x[:, e] = y
    k = rng.integers(0, 3, (N, 4, 1, K)); q[:, e] = np.where(k == 0, 0, np.where(k == 1, 255, q[:, e]))
    y = p[:, e]; y[..., ::5] = 0; p[:, e] = y
    th[:, e] = np.concatenate([rng.permutation(np.array([0, 1, 800, 900, 2000, 4080, 4081, 4096])) for a in range((N + 1) // 2)])[:4 * N].reshape(N, 4)
    return pack(x, q, p, mo, th)
def setup_inputs_alike(rng):
    x, q, p, mo, th = parts(rng)
    pool = rng.integers(0, H, (N, 8, 40)); pool[..., 0] = 0; pool[..., 1] = H - 1
    p = np.take_along_axis(pool, rng.integers(0, 40, (N, 8, 16 * V)), 2).reshape(N, 8, 16, V)
    q[:, :, :, 1::2] = q[:, :, :, 0::2]
    o = rng.permutation(8); i = np.arange(V)
    mo[:, o[0]] = i; mo[:, o[1]] = (i + 1) % V; mo[:, o[2]] = V - 1 - i
    return pack(x, q, p, mo, rng.integers(850, 1001, (N, 8)))
def setup_inputs_crowd(rng):
    x, q, p, mo, th = parts(rng)
    x = rng.integers(0, 96, x.shape); p = rng.integers(0, H - 2 * K, p.shape); th = rng.integers(400, 513, (N, 8))
    for a in range(0, N, 2):
        o = a + 1
        for g in range(8):
            hard = np.zeros(K, bool); hard[rng.permutation(K)[:CAP]] = True
            rec = rng.integers(0, H - 2 * K, K)
            w = x[a, g][:, rec] + rng.integers(0, 8, (16, K)); w[:, hard] = rng.integers(240, 256, (16, CAP))
            q[a, g] = w; u = start(w, 0)
            e = np.flatnonzero(~hard); p[a, g][rng.integers(0, 16, len(e)), u[e]] = rec[e]
            b = np.flatnonzero(hard); c = K * int(rng.integers(0, F))
            free = rng.permutation(np.setdiff1d(np.arange(c, c + K), u[b]))
            way = np.concatenate([u[b], free[:S * CAP]]).reshape(S + 1, CAP)
            mo[a, g] = mothers(rng, way[:-1].reshape(-1), way[1:].reshape(-1))
            x[o, g][:, H - K:H - K + CAP] = 8 * rng.integers(30, 32, (16, CAP))
            p[o, g][rng.integers(8, 16, CAP), way[S]] = H - K + np.arange(CAP)
            x[o, g][:, H - 2 * K:H - K] = rng.integers(136, 200, (16, K))
            if g % 2 == 0: rec = np.full(K, H - 2 * K)
            else:
                rec = H - 2 * K + rng.permutation(K); rec[K - 1] = rec[0]
            w = x[o, g][:, rec] + rng.integers(-8, 9, (16, K))
            q[o, g] = w; u = start(w, 0)
            free = rng.permutation(np.setdiff1d(np.arange(V), u))
            if g // 2 % 2 == 0: free = free[np.argsort(free // K != int(rng.integers(0, F)), kind="stable")]
            v = rng.permutation(free[:K]); mo[o, g] = mothers(rng, u, v)
            p[o, g][rng.integers(0, 8, K), v] = rec
    z = rng.integers(0, H, (N, 8, 1, 1))
    return pack(np.take_along_axis(x, (np.arange(H) - z) % H, 3), q, (p + z) % H, mo, th)
def setup_inputs_spread(rng):
    x, q, p, mo, th = parts(rng)
    x = np.minimum((np.exp2(8.2 * rng.random((N, 8, 1, H))) * rng.random((N, 8, 16, H))).astype(np.int64), 255)
    q = np.minimum((np.exp2(8.2 * rng.random((N, 8, 1, K))) * rng.random((N, 8, 16, K))).astype(np.int64), 255)
    return pack(x, q, p, mo, np.exp2(5 + 6 * rng.random((N, 8))).astype(np.int64))
def check_inputs(d):
    bad = []
    for k in ("x", "qs"):
        v = np.asarray(d[k]).astype(np.float64)
        if not np.all((v >= 0) & (v <= 255) & (v == np.floor(v))): bad.append("whole numbers from 0 to 255 in " + k)
    if np.min(d["towns"]) < 0 or np.max(d["towns"]) > H - 1: bad.append("range of towns")
    m = np.sort(np.asarray(d["mo"]), axis=-1)
    if not np.array_equal(m, np.broadcast_to(np.arange(V), m.shape)): bad.append("the mothers of a group are all different")
    t = np.asarray(d["th"]).reshape(-1, 16)
    if np.min(t) < 0 or np.max(t) > 4096: bad.append("range of th")
    if not np.all(t == t[:, :1]): bad.append("one threshold a group")
    return bad
def tries(rec, lists, u, q, th):
    li = np.take_along_axis(lists, u[:, None, :], 2)
    col = np.take_along_axis(rec, li.reshape(8, 1, 16 * K), 2).reshape(8, 16, 16, K)
    dist = np.add.reduce(np.abs(col - q[:, :, None, :]), axis=1)
    best = np.argmin(dist, axis=1); worst = np.argmax(dist, axis=1)
    num = np.take_along_axis(li, best[:, None, :], 1)[:, 0]
    return np.min(dist, axis=1) < th[:, None], num, worst, li
def reference(x, qs, towns, mo, th):
    X = np.zeros((N, 8, 16, W), np.int32); X[..., :H] = x.astype(np.float32).astype(np.int32).reshape(N, 8, 16, H)
    q = qs.astype(np.float32).astype(np.int32).reshape(N, 8, 16, K)
    P = towns.astype(np.int64).reshape(N, 8, 16, V); M = mo.astype(np.int64); T = th.reshape(N, 8, 16)[:, :, 0].astype(np.int64)
    ans = np.zeros((N, K), np.int64)
    for t in range(R):
        X1, P1, M1, q1, ans1 = X.copy(), P.copy(), M.copy(), q.copy(), ans.copy()
        for a in range(N):
            u = start(q[a].astype(np.int64), ans[a][None, :]); home = np.zeros((8, K), bool); num = np.zeros((8, K), np.int64); path = []
            for s in range(S):
                ok, nm, worst, li = tries(X[a], P[a], u, q[a], T[a])
                hit = ok & ~home; fail = ~ok & ~home
                num = np.where(hit, nm, num); path.append((u, fail, worst, li)); home = home | hit
                u = np.where(fail, np.take_along_axis(M[a], u, 1), u)
            slot = np.add.accumulate((~home).astype(np.int64), axis=1) - 1; place = H + CAP * t + slot
            o = (a + 1 + t) % N
            ok, nm, worst, li = tries(X[o], P[o], u, q[a], T[o])
            came = ok & ~home & (slot < CAP); got = home | came
            old = np.where(home[:, None, :], np.take_along_axis(X[a], num[:, None, :], 2), np.take_along_axis(X[o], nm[:, None, :], 2))
            num = np.where(came, place, num)
            for g in range(8):
                for u_, fail, worst, li in path[::-1]:
                    j = np.flatnonzero(fail[g] & got[g]); new = li[g][:, j]; new[worst[g, j], np.arange(len(j))] = num[g, j]
                    P1[a, g][:, u_[g, j]] = new
                u0, f0 = path[0][0][g], path[0][1][g]
                k = np.flatnonzero(f0[0::2] & f0[1::2]); v, w = u0[2 * k], u0[2 * k + 1]
                M1[a, g, v] = M[a, g, w]; M1[a, g, w] = M[a, g, v]
                j = np.flatnonzero(home[g]); r, i = np.unique(num[g, j], return_index=True); j = j[i]
                X1[a, g][:, r] = (X[a, g][:, r] + q[a, g][:, j]) >> 1
                j = np.flatnonzero(came[g]); X1[a, g][:, place[g, j]] = old[g][:, j]
            q1[a] = np.where(got[:, None, :], (q[a] + old) & 255, q[a])
            ans1[a] = np.add.reduce(got.astype(np.int64), axis=0)
        X, P, M, q, ans = X1, P1, M1, q1, ans1
    return {"yx": X.reshape(N, 128, W).astype(np.float32).astype(BF), "yp": P.reshape(N, 128, V).astype(np.float32), "ym": M.astype(np.float32)}

@@ -1,0 +1,571 @@
+import numpy as np
+from concourse.mybir import AluOpType as A, ActivationFunctionType as AF
+
+R_, H, V, K, CAP, N = 3, 2624, 512, 256, 64, 8
+PAD, W = 16, 2816
+TRX, TRP = PAD + W, V
+BIG = float(2 ** 30)
+ENG = 8
+QA = 6
+
+BUF, AT = {}, {}
+SCRATCH = {}
+
+
+def _add(where, dtype, **kw):
+    for k, v in kw.items():
+        BUF[k] = (where, [128] + (v if isinstance(v, list) else [v]), dtype)
+        SCRATCH["z_" + k] = BUF[k]
+
+
+def _pack(dtype, **kw):
+    at = 0
+    for k, v in kw.items():
+        BUF[k] = ("sbuf", [128, v], dtype)
+        AT[k] = ("t_" + dtype, at, v)
+        at += (v + 15) // 16 * 16
+    SCRATCH["t_" + dtype] = ("sbuf", [128, at], dtype)
+
+
+_add("sbuf", "int32", pti=V, moi=V, thi=1, vv=256, pk0=256, pk1=256, pk2=256, pkr0=64, pkr1=64, pkr2=64, sh=256, rn=256, qh=256,
+     s1=256, s2=256)
+_pack("int32", pc=1, pmi=1, pgi=1, podd=1, bi=16, bq=16, kc=32, ke=32, wi=32, we=32, u2i=64, qi=64, gkc=4, gpos=4)
+_add("sbuf", "uint16", li=512)
+_pack("uint16", uu=32, offu=16, numu=16, xoff=32, poff=32, u2u=4, posu=4, lig=64, expl=16)
+_add("sbuf", "bfloat16", x=TRX + 256, q=256, qrep=4096, d=8192, xg=1024, ad=[32, 16, 16], lm=[16, 128], wem=[16, 128], bm=[16, 128],
+     ci=256, c2=256, resn=256, resx=256, nt=256, qg=1024, dg=1040, adg=[4, 16, 16], rs0=64, rs1=64, rs2=64, rr0=64, rr1=64, rr2=64)
+_pack("bfloat16", id=128, nid=128, bo=128, nbo=128, ntri=128, id14=128, sw=128, swd=128, sg=128, one=128, tmpb=128, ef=256, it=256,
+      dm=256, trib=256, resa=256, wm=512, e=256, fw=256, gw=256, c=256, jb=16, rj=16, zz=16, okt=32, h=16, f0=16, un=16, hj=16, cs=32,
+      ewa=32, ewb=32, xk=16, cap=64, qb=64, rz=64, got=16)
+_add("sbuf", "float16", moh=[16, 2], mo8=[16, 32], e8=128, pcg=64)
+_pack("float16", lic=512, ns=512, pl=32, u1h=16)
+_add("sbuf", "float32", pt=V + 256, m256=V, pf=1, sc=512, sw2=512, sg2=64, ym2=V, mt=256)
+_pack("float32", pm=1, pg=1, pidx=1, widx=1, evc=1, th32=1, th2k=1, dcol=16, idf=128, j2=16, trx=16, trp=32, ios=64, dmo=16, uf=32,
+      t16=16, dl=16, d1=16, d0=16, capf=64, wd=512, kw=512, plf=16, numf=16, nrb=256, cnt=256, l0=16, lt=16, xo=16, nl=512, um=64,
+      us=64, du=32, vf=32, pz=32, po=32, ms=256)
+_add("psum", "float32", b0=512, b1=512, b2=512, b3=512, b4=[16, 32], b5=512, b6=512, b7=512)
+SEMAPHORES = ["sv", "sa", "st", "sg", "loc"] + ["dma%d" % i for i in range(16)] + ["rq%d" % t for t in range(3)] + ["rp%d" % t for t in range(3)]
+
+
+def _emask(topo, src, dst, n):
+    m = 0
+    for e in topo.engines(src, dst)[:n]:
+        m |= 1 << e
+    return m
+
+
+def _relay(topo, src, dst):
+    if topo.may_write(src, dst):
+        return None
+    for c in topo.cores_of(src):
+        if topo.die(c) == topo.die(src) and topo.may_write(c, dst):
+            return c
+    return None
+
+
+def _send(g, T, topo, src, dst, name, sem, cols=None):
+    rid, pid = topo.addr(dst, src)
+    ap_out = T["z_" + name][:] if cols is None else T["z_" + cols[0]][:]
+    ap_in = T["z_" + name][:] if cols is None else T["z_" + name][:, 0:cols[1]]
+    g.remote_dma(ap_out, ap_in, T.sem[sem], T.sem.loc, pid, rid, _emask(topo, src, dst, ENG))
+    return len(topo.engines(src, dst)[:ENG])
+
+
+def _hand_on(g, core, T, topo):
+    n = 0
+    for t in range(R_):
+        for kind in ("rq", "rp"):
+            for r in range(N):
+                a, b = T.cores[r], T.cores[(r + 1 + t) % N]
+                src, dst = (a, b) if kind == "rq" else (b, a)
+                if _relay(topo, src, dst) == core:
+                    g.wait_ge(T.sem["%s%d" % (kind, t)], len(topo.engines(src, core)[:ENG]))
+                    n += _send(g, T, topo, core, dst, ("pkr%d" if kind == "rq" else "rr%d") % t, "%s%d" % (kind, t))
+    if n:
+        g.wait_ge(T.sem.loc, n)
+
+
+def rank_program(g, core, T, topo):
+    rank = T.rank_of(core)
+    if rank is None:
+        _hand_on(g, core, T, topo)
+        return
+
+    Q = {"v": g.vector, "s": g.scalar, "t": g.tensor, "g": g, "y": g.sync}
+    SEM = {"v": "sv", "s": "sa", "t": "st", "g": "sg"}
+    total, hist, clk, known, cache = {}, {}, {}, {k: {} for k in "vstgy"}, {}
+    ndma = [0]
+
+    def B(name, *idx):
+        key = (name, idx)
+        if key not in cache:
+            full = (slice(None),) + tuple(slice(*i) if isinstance(i, tuple) else i for i in idx)
+            m = np.zeros(BUF[name][1][1:], bool)
+            m[tuple(full[1:])] = True
+            if name in AT:
+                phys, at, w = AT[name]
+                lo, hi, st = (tuple(idx[0]) + (1,))[:3] if idx else (0, w, 1)
+                ap = T[phys][:, at + lo:at + hi:st] if st > 1 else T[phys][:, at + lo:at + hi]
+            else:
+                ap = T["z_" + name][full]
+            cache[key] = (ap, name, int.from_bytes(np.packbits(m.ravel(), bitorder="little").tobytes(), "little"))
+        return cache[key]
+
+    def deps(q, reads, writes):
+        need = {}
+
+        def want(rec):
+            need[rec[2]] = max(need.get(rec[2], 0), rec[3])
+        for wr, lst in ((False, reads), (True, writes)):
+            for ap, name, m in lst:
+                ps = BUF[name][0] == "psum"
+                for rec in hist.get(name, ()):
+                    same = rec[4] == q
+                    if ps and not same:
+                        want(rec)
+                    elif rec[0] & m:
+                        if rec[1] and not (ps and q == "t" and same):
+                            want(rec)
+                        elif wr and not rec[1] and not same:
+                            want(rec)
+        return need
+
+    def wait(q, need):
+        kn = known[q]
+        todo = {s: v for s, v in need.items() if kn.get(s, 0) < v}
+        for s, v in todo.items():
+            if any(o != s and clk[(o, w)].get(s, 0) >= v for o, w in todo.items()):
+                continue
+            if kn.get(s, 0) >= v:
+                continue
+            Q[q].wait_ge(T.sem[s], v)
+            for k2, v2 in clk[(s, v)].items():
+                kn[k2] = max(kn.get(k2, 0), v2)
+            kn[s] = max(kn.get(s, 0), v)
+
+    def record(q, reads, writes, sem, val):
+        clk[(sem, val)] = dict(known[q])
+        for ap, name, m in writes:
+            hist[name] = [r for r in hist.get(name, []) if r[0] & ~m] + [(m, True, sem, val, q)]
+        for ap, name, m in reads:
+            hist[name] = [r for r in hist.get(name, []) if r[1] or r[4] != q or r[0] & ~m] + [(m, False, sem, val, q)]
+
+    def op(q, fn, out, *ins):
+        wait(q, deps(q, ins, (out,)))
+        sem = SEM[q]
+        total[sem] = total.get(sem, 0) + 1
+        fn().then_inc(T.sem[sem], 1)
+        record(q, ins, (out,), sem, total[sem])
+
+    def dma(q, out, in_, reads, writes):
+        wait(q, deps(q, reads, writes))
+        sem = "dma%d" % ndma[0]
+        ndma[0] += 1
+        total[sem] = 16
+        Q[q].dma_start(out, in_).then_inc(T.sem[sem], 16)
+        record(q, reads, writes, sem, 16)
+
+    def arrived(name, sem, src, dst):
+        n = len(topo.engines(src, dst)[:ENG])
+        total[sem] = n
+        clk[(sem, n)] = {}
+        hist[name] = [((1 << 64) - 1, True, sem, n, "r")]
+
+    vec, act, pe = g.vector, g.scalar, g.tensor
+
+    def cp(out, in_):
+        op("v", lambda: vec.tensor_copy(out[0], in_[0]), out, in_)
+
+    def tt(out, a, b, o):
+        op("v", lambda: vec.tensor_tensor(out[0], a[0], b[0], o), out, a, b)
+
+    def ts(out, a, s1, o1, s2=None, o2=None):
+        cols = [s for s in (s1, s2) if isinstance(s, tuple)]
+        x1 = s1[0] if isinstance(s1, tuple) else s1
+        x2 = s2[0] if isinstance(s2, tuple) else s2
+        if o2 is None:
+            op("v", lambda: vec.tensor_scalar(out[0], a[0], x1, None, o1), out, a, *cols)
+        else:
+            op("v", lambda: vec.tensor_scalar(out[0], a[0], x1, x2, o1, o2), out, a, *cols)
+
+    def scan(out, d0, d1, o1, o2):
+        op("v", lambda: vec.tensor_tensor_scan(out[0], d0[0], d1[0], 0.0, o1, o2), out, d0, d1)
+
+    def gat(out, win, off):
+        op("v", lambda: vec.tensor_copy(out[0], win[0].indirect(off[0])), out, win, off)
+
+    def gat_tt(out, win, off, b, o):
+        op("v", lambda: vec.tensor_tensor(out[0], win[0].indirect(off[0]), b[0], o), out, win, off, b)
+
+    def scat(win, off, in_):
+        op("v", lambda: vec.tensor_copy(win[0].indirect(off[0]), in_[0]), win, off, in_)
+
+    def fill(out, c):
+        op("v", lambda: vec.memset(out[0], c), out)
+
+    def ac(out, in_, f, bias=0.0, scale=1.0):
+        if isinstance(scale, tuple):
+            op("s", lambda: act.activation(out[0], in_[0], f, bias=bias, scale=scale[0]), out, in_, scale)
+        else:
+            op("s", lambda: act.activation(out[0], in_[0], f, bias=bias, scale=scale), out, in_)
+
+    def agat(out, win, off, bias=0.0, scale=1.0):
+        op("s", lambda: act.activation(out[0], win[0].indirect(off[0]), AF.Identity, bias=bias, scale=scale), out, win, off)
+
+    def mm(out, l, r, start, stop):
+        op("t", lambda: pe.matmul(out[0], l[0], r[0], start, stop), out, l, r)
+
+    def iota(out, pattern, base=0, mult=0):
+        if BUF[out[1]][2] == "int32":
+            op("g", lambda: g.iota(out[0], pattern, base, mult), out)
+        else:
+            op("g", lambda: g.iota(out[0], pattern, base, mult, allow_small_or_imprecise_dtypes=True), out)
+
+    def send(dst, name, sem, cols=None):
+        hop = _relay(topo, core, dst)
+        src = B(name) if cols is None else B(name, (0, cols[1]))
+        wait("g", deps("g", (src,), ()))
+        n = _send(g, T, topo, core, dst if hop is None else hop, name, sem, cols)
+        total["loc"] = total.get("loc", 0) + n
+
+    dma("y", B("q")[0], T.qs[:], (), (B("q"),))
+    dma("s", B("x", (PAD, PAD + H))[0], T.x[:], (), (B("x", (PAD, PAD + H)),))
+    dma("y", B("pti")[0], T.towns[:], (), (B("pti"),))
+    dma("y", T.z_moi[0:8, :], T.mo[:], (), (B("moi"),))
+    dma("y", B("thi")[0], T.th[:], (), (B("thi"),))
+    AND, SHR = A.bitwise_and, A.arith_shift_right
+    iota(B("pc"), [[1, 1]], 0, 1)
+    iota(B("nt"), [[1, 16], [0, 16]])
+    iota(B("it"), [[0, 16], [1, 16]])
+    iota(B("ef"), [[1, 256]])
+    fill(B("lm"), 0.0)
+    fill(B("one"), 1.0)
+    op("g", lambda: g.affine_select(B("id")[0], B("one")[0], [[-1, 128]], A.is_equal, 0.0, 0, 1), B("id"), B("one"))
+    iota(B("ci"), [[0, 16], [1, 16]], 1)
+    iota(B("c2"), [[0, 16], [-2, 16]], -2)
+    iota(B("ios"), [[1, 64]])
+    ts(B("pmi"), B("pc"), 15, AND)
+    ts(B("pgi"), B("pc"), 4, SHR)
+    ts(B("podd"), B("pc"), 1, AND)
+    cp(B("pg"), B("pgi"))
+    ts(B("evc"), B("podd"), -1.0 / 32, A.mult, 1.0 / 32, A.add)
+    cp(B("pm"), B("pmi"))
+    cp(B("pf"), B("pc"))
+    e128, i128, n128 = B("ef", (0, 128)), B("it", (0, 128)), B("nt", (0, 128))
+    ts(B("bo"), n128, B("pg"), A.is_equal)
+    for m in range(16):
+        ac(B("lm", m, (m, 128, 16)), B("bo", (m, 128, 16)), AF.Copy, scale=32.0)
+    ts(B("resn"), B("it"), 0.5, A.is_lt, 2 * BIG, A.mult)
+    ts(B("resn"), B("resn"), -BIG, A.add)
+    ts(B("j2"), B("ef", (0, 16)), 16.0, A.mult, B("pm"), A.add)
+    cp(B("jb"), B("j2"))
+    ts(B("rj"), B("j2"), -1.0, A.mult, 255.0, A.add)
+    ts(B("trx"), B("j2"), float(TRX), A.add)
+    for s in range(2):
+        ts(B("trp", (16 * s, 16 * s + 16)), B("j2"), float(TRP), A.add)
+    ts(B("j2"), B("j2"), 2.0, A.mult)
+    ts(B("nid"), e128, B("pf"), A.is_equal, -1.0, A.mult)
+    fill(B("x", (0, PAD)), 0.0)
+    fill(B("x", (PAD + H, TRX)), 0.0)
+
+    def qrep_v(lo, hi):
+        for i in range(lo, hi):
+            cp(B("qrep", (i, 4096, 16)), B("q"))
+
+    def qrep_s():
+        for i in range(16 - QA, 16):
+            ac(B("qrep", (i, 4096, 16)), B("q"), AF.Copy)
+
+    def parity(last):
+        for m in range(16):
+            mm(B("b6", (0, 16)), B("wem", m), B("q", (m, 256, 16)), m == 0, last and m == 15)
+
+    qrep_v(0, 5)
+    ts(B("wem"), B("lm"), B("evc"), A.mult)
+    parity(True)
+    qrep_s()
+    qrep_v(5, 16 - QA)
+    cp(B("pt", (0, V)), B("pti"))
+
+    def first_mothers():
+        op("v", lambda: vec.tensor_copy(T.z_mo8[0:8, :, :], T.z_moi[0:8, :]), B("mo8"), B("moi"))
+        op("v", lambda: vec.tensor_scalar(T.z_e8[0:8, :], T.z_nt[0:8, 0:128], T.z_pf[0:8, 0:1], None, A.is_equal), B("e8"), B("nt"), B("pf"))
+        op("t", lambda: pe.matmul(B("b4")[0], T.z_e8[0:8, :], T.z_mo8[0:8, :, :], True, True), B("b4"), B("e8"), B("mo8"))
+        ts(B("dm"), B("it"), B("pm"), A.is_equal)
+        ts(B("resa"), B("it"), 0.5, A.is_gt)
+        for s in range(2):
+            tt(B("mt"), B("b4", (0, 16), (s, 32, 2)), B("dm"), A.mult)
+            scan(B("ms"), B("resa"), B("mt"), A.mult, A.add)
+            cp(B("moh", (0, 16), s), B("ms", (15, 256, 16)))
+        tt(B("dmo"), B("moh", (0, 16), 1), B("moh", (0, 16), 0), A.subtract)
+
+    def late_constants():
+        ts(B("dcol"), B("ef", (0, 16)), B("pm"), A.is_equal)
+        ts(B("resx"), B("resn"), -1.0, A.mult)
+        ts(B("th32"), B("thi"), 32.0, A.mult)
+        ts(B("th2k"), B("thi"), 2048.0, A.mult)
+        ts(B("nbo"), B("bo"), -1.0, A.mult)
+        ts(B("tmpb"), i128, B("pm"), A.is_gt, -1.0, A.mult)
+        tt(B("ntri"), B("tmpb"), B("bo"), A.mult)
+        ts(B("id14"), B("id"), 1424.0, A.mult)
+        ts(B("t16", (0, 1)), B("podd"), -2.0, A.mult, 1.0, A.add)
+        tt(B("t16", (0, 1)), B("t16", (0, 1)), B("pf"), A.add)
+        ts(B("sw"), e128, B("t16", (0, 1)), A.is_equal)
+        tt(B("swd"), B("sw"), B("id"), A.subtract)
+        ts(B("sg"), i128, B("pm"), A.is_equal)
+        fill(B("zz"), 0.0)
+        fill(B("cs"), 0.0)
+        ts(B("trib"), B("it"), B("pm"), A.is_ge, 1024.0, A.mult)
+        ts(B("pidx"), B("pm"), 1.0, A.add)
+        ts(B("widx"), B("pm"), -1.0, A.mult, 31.0, A.add)
+        cp(B("expl"), B("ios", (0, 16)))
+        ts(B("t16", (0, 1)), B("pm"), 16.0, A.mult, 16.0, A.add)
+        ts(B("um"), B("nt", (0, 64)), 256.0, A.mult, B("t16", (0, 1)), A.add)
+        tt(B("pcg"), B("um"), B("it", (0, 64)), A.add)
+        fill(B("dg", (0, 16)), -512.0)
+        fill(B("fw", (64, 256)), 0.0)
+        fill(B("gw", (64, 256)), 0.0)
+        cp(B("idf"), B("id"))
+
+    xwin = B("x", (PAD, TRX))
+    u0, u1 = B("uf", (0, 16)), B("uf", (16, 32))
+    k0, k1 = B("b0", (0, 256)), B("b1", (0, 256))
+    best0, best1 = B("sc", (15, 256, 16)), B("sc", (271, 512, 16))
+
+    for t in range(R_):
+        end = t == R_ - 1
+        guest, host_of = T.cores[(rank - 1 - t) % N], T.cores[(rank + 1 + t) % N]
+        pk, pkr, rs, rr = "pk%d" % t, "pkr%d" % t, "rs%d" % t, "rr%d" % t
+
+        def came_from(src):
+            hop = _relay(topo, src, core)
+            return src if hop is None else hop
+
+        def diff(k, parts=(0, 1)):
+            lo, hi = 2 * k + parts[0], 2 * k + parts[-1] + 1
+            r = lo % 8
+            gat_tt(B("d", (512 * lo, 512 * hi)), xwin, B("li", (32 * lo, 32 * hi)), B("qrep", (512 * r, 512 * (r + hi - lo))), A.subtract)
+
+        def absd(k, parts=(0, 1)):
+            lo, hi = 2 * k + parts[0], 2 * k + parts[-1] + 1
+            ac(B("ad", (2 * lo, 2 * hi)), B("d", (512 * lo, 512 * hi)), AF.Abs)
+
+        def reduce(k):
+            s, c = k // 4, k % 4
+            out = B("b%d" % s, (64 * c, 64 * c + 64))
+            mm(out, B("id"), B("ci", (64 * c, 64 * c + 64)), True, False)
+            for m in range(16):
+                mm(out, B("lm", m), B("ad", (4 * k, 4 * k + 4), m), False, m == 15)
+
+        cp(B("bi"), B("b6", (0, 16)))
+        ts(B("bq"), B("bi"), 1, AND)
+        tt(u0, B("bq"), B("j2"), A.add)
+
+        def second_town():
+            tt(B("t16"), B("bq"), B("dmo"), A.mult)
+            tt(u1, B("t16"), B("moh", (0, 16), 0), A.add)
+
+        if t == 0:
+            cp(B("uu", (0, 16)), u0)
+            gat(B("li", (0, 256)), B("pt", (0, V)), B("uu", (0, 16)))
+        else:
+            second_town()
+            cp(B("uu"), B("uf"))
+            gat(B("li"), B("pt", (0, V)), B("uu"))
+        agat(B("xg"), xwin, B("li", (0, 64)))
+        for a in range(2):
+            mm(B("b%d" % (2 + a)), B("nid"), B("qrep", (512 * a, 512 * a + 512)), True, False)
+            mm(B("b%d" % (2 + a)), B("id"), B("xg", (512 * a, 512 * a + 512)), False, True)
+            ac(B("ad", (2 * a, 2 * a + 2)), B("b%d" % (2 + a)), AF.Abs)
+        diff(1)
+        absd(1)
+        if t == 0:
+            first_mothers()
+            second_town()
+            cp(B("uu", (16, 32)), u1)
+            gat(B("li", (256, 512)), B("pt", (0, V)), B("uu", (16, 32)))
+        reduce(0)
+        reduce(1)
+        diff(2)
+        if t == 0:
+            ac(B("m256"), B("b4"), AF.Copy, scale=256.0)
+        absd(2)
+        reduce(2)
+        diff(3)
+        absd(3)
+        reduce(3)
+        diff(4)
+        absd(4)
+        reduce(4)
+        if t == 0:
+            late_constants()
+        gat_tt(B("vv"), B("m256"), B("uu", (16, 32)), B("q"), A.add)
+        tt(B("du"), B("uf"), B("trp"), A.subtract)
+        cp(B("u1h"), u1)
+        diff(5)
+        absd(5)
+        reduce(5)
+        scan(B("sc", (0, 256)), B("resn"), k0, A.max, A.min)
+        ts(B("okt", (0, 16)), best0, B("th32"), A.is_lt)
+        ts(B("f0"), B("okt", (0, 16)), -1.0, A.mult, 1.0, A.add)
+        diff(6)
+        absd(6)
+        mm(B("b6", (48, 64)), B("swd"), B("u1h"), True, True)
+        mm(B("b6", (64, 80)), B("sw"), B("f0"), True, True)
+        reduce(6)
+        for hf in range(2):
+            diff(7, (hf,))
+            absd(7, (hf,))
+        reduce(7)
+        tt(B("xk"), B("b6", (64, 80)), B("f0"), A.mult)
+        tt(B("dl"), B("b6", (48, 64)), B("xk"), A.mult)
+        tt(B("kw", (0, 256)), k0, B("c2"), A.add)
+        scan(B("sw2", (0, 256)), B("resx"), B("kw", (0, 256)), A.min, A.max)
+        tt(B("d1"), B("dl"), B("bq"), A.mult)
+        tt(B("d0"), B("dl"), B("d1"), A.subtract)
+        tt(B("moh", (0, 16), 1), B("moh", (0, 16), 1), B("d1"), A.add)
+        tt(B("moh", (0, 16), 0), B("moh", (0, 16), 0), B("d0"), A.add)
+        ts(B("kc", (0, 16)), best0, B("th32"), A.min)
+        ts(B("ke", (0, 16)), B("kc", (0, 16)), 31, AND)
+        cp(B("ewa", (0, 16)), B("ke", (0, 16)))
+        tt(B("dmo"), B("moh", (0, 16), 1), B("moh", (0, 16), 0), A.subtract)
+        scan(B("sc", (256, 512)), B("resn"), k1, A.max, A.min)
+        ts(B("okt", (16, 32)), best1, B("th32"), A.is_lt)
+        tt(B("h"), B("okt", (0, 16)), B("okt", (16, 32)), A.max)
+        scan(B("cs", (1, 17)), B("h"), B("zz"), A.add, A.add)
+        tt(B("hj"), B("h"), B("rj"), A.mult)
+        off = B("b6", (16, 32))
+        mm(off, B("id"), B("jb"), True, False)
+        mm(off, B("ntri"), B("h"), False, False)
+        mm(off, B("nbo"), B("cs", (0, 16)), False, False)
+        mm(off, B("id"), B("hj"), False, True)
+        ts(B("kc", (16, 32)), best1, B("th32"), A.min)
+        ts(B("ke", (16, 32)), B("kc", (16, 32)), 31, AND)
+        tt(B("ewa", (16, 32)), B("ke", (16, 32)), B("f0"), A.mult)
+        ts(B("un"), B("h"), -1.0, A.mult, 1.0, A.add)
+        mm(B("b6", (32, 33)), B("bo"), B("cs", (16, 17)), True, True)
+        cp(B("offu"), off)
+        scat(B(pk, (0, 256)), B("offu"), B("vv"))
+        send(host_of, pk, "rq%d" % t, (pkr, 64))
+        agat(B("lic"), B("pt", (0, V)), B("uu"), bias=-44.0, scale=1.0 / 32)
+        if t == 0:
+            for m in range(16):
+                ac(B("bm", m), B("bo"), AF.Copy, scale=B("dcol", (m, m + 1)))
+        for m in range(16):
+            mm(B("b2", (m, 512, 16)), B("bm", m), B("ewa"), True, True)
+        tt(B("kw", (256, 512)), k1, B("c2"), A.add)
+        ts(B("plf"), off, 1.0 / 32, A.mult, (1216.0 + 64 * t) / 32, A.add)
+        for s in range(2):
+            tt(B("pl", (16 * s, 16 * s + 16)), B("plf"), B("un"), A.mult)
+        ts(B("capf"), B("ios"), B("b6", (32, 33)), A.add, 256.0, A.is_lt)
+        ts(B("cap"), B("capf"), 256.0, A.mult, -1.0, A.add)
+        ts(B("b3"), B("b2"), B("pidx"), A.is_equal)
+        tt(B("ns"), B("b3"), B("lic"), A.mult)
+        scan(B("sw2", (256, 512)), B("resx"), B("kw", (256, 512)), A.min, A.max)
+        ts(B("wi"), B("sw2", (15, 512, 16)), -64.0, A.max)
+        ts(B("we"), B("wi"), 31, AND)
+        cp(B("ewb"), B("we"))
+        num = B("b6", (80, 96))
+        for m in range(16):
+            for s in range(2):
+                mm(num, B("lm", m), B("ns", (256 * s + m, 256 * s + 256, 16)), m == 0 and s == 0, False)
+        mm(num, B("id14"), B("h"), False, True)
+        for m in range(16):
+            mm(B("b4", (0, 16), (2 * m, 2 * m + 2)), B("bm", m), B("moh"), True, True)
+        for m in range(16):
+            mm(B("b7", (m, 512, 16)), B("bm", m), B("ewb"), True, True)
+        mm(B("b5"), B("nid"), B("lic"), True, False)
+        for s in range(2):
+            for s2 in range(2):
+                mm(B("b5", (256 * s, 256 * s + 256)), B("bo"), B("ns", (256 * s2, 256 * s2 + 256)), False, False)
+        for m in range(16):
+            mm(B("b5", (m, 512, 16)), B("bm", m), B("pl"), False, m == 15)
+        cp(B("numu"), num)
+        cp(B("numf"), num)
+        gat_tt(B("sh"), B("x", (0, TRX)), B("numu"), B("q"), A.add)
+        ts(B("rn"), B("sh"), 1, SHR)
+        if not end:
+            ts(B("qh"), B("sh"), 255, AND)
+        arrived(pkr, "rq%d" % t, came_from(guest), core)
+        ts(B("u2i"), B(pkr), 8, SHR)
+        tt(B("um"), B("u2i"), B("dm", (0, 64)), A.mult)
+        scan(B("us"), B("resa", (0, 64)), B("um"), A.mult, A.add)
+        ts(B("qi"), B(pkr), 255, AND)
+        cp(B("u2u"), B("us", (15, 64, 16)))
+        cp(B("qb"), B("qi"))
+        gat(B("lig"), B("pt", (0, V)), B("u2u"))
+        for i in range(8):
+            ac(B("qg", (8 + i, 1024, 16)), B("qb"), AF.Copy)
+            cp(B("qg", (i, 1024, 16)), B("qb"))
+        for hf in range(2):
+            gat_tt(B("dg", (16 + 512 * hf, 528 + 512 * hf)), xwin, B("lig", (32 * hf, 32 * hf + 32)), B("qg", (512 * hf, 512 * hf + 512)), A.subtract)
+            ac(B("adg", (2 * hf, 2 * hf + 2)), B("dg", (16 + 512 * hf, 528 + 512 * hf)), AF.Abs, scale=64.0)
+        gk = B("b1", (0, 64))
+        mm(gk, B("id"), B("pcg"), True, False)
+        for m in range(16):
+            mm(gk, B("lm", m), B("adg", (0, 4), m), False, m == 15)
+        ts(B("wm"), B("b7"), B("widx"), A.is_equal)
+        tt(B("wd"), B("b5"), B("wm"), A.mult)
+        scan(B("sg2"), B("resn", (0, 64)), gk, A.max, A.min)
+        ts(B("gkc"), B("sg2", (15, 64, 16)), B("th2k"), A.min)
+        ts(B("gpos"), B("gkc"), 2047, AND)
+        cp(B("posu"), B("gpos"))
+        gat_tt(B(rs), B("dg"), B("posu"), B("qb"), A.add)
+        send(guest, rs, "rp%d" % t, (rr, 64))
+        nr = B("b2", (0, 256))
+        mm(nr, B("id"), B("trib"), True, False)
+        for s in range(2):
+            mm(nr, B("bo"), B("ns", (256 * s, 256 * s + 256)), False, False)
+        for m in range(16):
+            mm(B("b2", (m, 256, 16)), B("bm", m), B("pl", (0, 16)), False, m == 15)
+        ac(B("nrb"), nr, AF.Identity, bias=1424.0, scale=32.0)
+        mm(B("b7"), B("id"), B("lic"), True, False)
+        mm(B("b7"), B("idf"), B("wd"), False, True)
+        if not end:
+            ac(B("m256"), B("b4"), AF.Copy, scale=256.0)
+        else:
+            ac(B("ym2"), B("b4"), AF.Copy)
+            dma("y", T.ym[:], T.z_ym2[0:128:16, :], (B("ym2"),), ())
+        ac(B("nl"), B("b7"), AF.Identity, bias=1408.0, scale=32.0)
+        gat_tt(B("e"), B("numf"), B("expl"), B("nrb"), A.is_equal)
+        scan(B("cnt"), B("resa"), B("e"), A.mult, A.add)
+        ts(B("l0"), B("cnt", (15, 256, 16)), 0.5, A.is_ge)
+        tt(B("l0"), B("l0"), B("un"), A.max)
+        tt(B("lt"), B("l0"), B("trx"), A.mult)
+        tt(B("xo"), B("lt"), B("numf"), A.max)
+        cp(B("xoff", (0, 32, 2)), B("xo"))
+        for n in range(15, -1, -1):
+            scat(B("x"), B("xoff", (2 * n, 2 * n + 1)), B("rn", (16 * n, 16 * n + 16)))
+        if end:
+            dma("y", T.yx[:, 0:H + 2 * CAP], B("x", (PAD, PAD + H + 2 * CAP))[0], (B("x", (PAD, PAD + H + 2 * CAP)),), ())
+        arrived(rr, "rp%d" % t, came_from(host_of), core)
+        tt(B("rz"), B(rr), B("cap"), A.min)
+        ts(B("fw", (0, 64)), B("rz"), 0.0, A.is_ge, 1.0 / 512, A.mult)
+        agat(B("c"), B("fw"), B("offu"))
+        ts(B("gw", (0, 64)), B("rz"), 0.0, A.max)
+        gcol = B("x", (PAD + H + CAP * t, PAD + H + CAP * t + CAP))
+        came = B("b6", (96, 112))
+        for m in range(16):
+            mm(came, B("lm", m), B("c", (m, 256, 16)), m == 0, m == 15)
+        if not end:
+            gat_tt(B("s1"), B("gw"), B("offu"), B("qh"), A.add)
+            ts(B("s2"), B("s1"), 255, AND)
+            cp(B("q"), B("s2"))
+            parity(False)
+            qrep_s()
+            qrep_v(0, 16 - QA)
+        ac(gcol, B("gw", (0, 64)), AF.Copy)
+        tt(B("got"), B("h"), came, A.max)
+        cp(B("vf", (16, 32)), came)
+        if not end:
+            mm(B("b6", (0, 16)), B("sg"), B("got"), False, True)
+        tt(B("vf", (0, 16)), B("got"), B("f0"), A.mult)
+        tt(B("pz"), B("vf"), B("du"), A.mult)
+        tt(B("po"), B("pz"), B("trp"), A.add)
+        cp(B("poff"), B("po"))
+        scat(B("pt"), B("poff", (16, 32)), B("nl", (256, 512)))
+        scat(B("pt"), B("poff", (0, 16)), B("nl", (0, 256)))
+    dma("y", T.yx[:, H + 2 * CAP:W], B("x", (PAD + H + 2 * CAP, TRX))[0], (B("x", (PAD + H + 2 * CAP, TRX)),), ())
+    dma("s", T.yp[:], B("pt", (0, V))[0], (B("pt", (0, V)),), ())
+    for s, v in total.items():
+        g.wait_ge(T.sem[s], v)

@@ -6,7 +6,7 @@ PAD, W = 16, 2816
 TRX, TRP = PAD + W, V
 BIG = float(2 ** 30)
 ENG = 8
-QA = 6
+QA = 10
 
 BUF, AT = {}, {}
 SCRATCH = {}
@@ -27,22 +27,22 @@ def _pack(dtype, **kw):
     SCRATCH["t_" + dtype] = ("sbuf", [128, at], dtype)
 
 
-_add("sbuf", "int32", pti=V, moi=V, thi=1, vv=256, pk0=256, pk1=256, pk2=256, pkr0=64, pkr1=64, pkr2=64, sh=256, rn=256, qh=256,
+_add("sbuf", "int32", pti=V, moi=V, thi=1, vv=256, pk0=256, pk1=256, pk2=256, pkr0=64, pkr1=64, pkr2=64, sh=256, rn=256,
      s1=256, s2=256)
 _pack("int32", pc=1, pmi=1, pgi=1, podd=1, bi=16, bq=16, kc=32, ke=32, wi=32, we=32, u2i=64, qi=64, gkc=4, gpos=4)
 _add("sbuf", "uint16", li=512)
 _pack("uint16", uu=32, offu=16, numu=16, xoff=32, poff=32, u2u=4, posu=4, lig=64, expl=16)
 _add("sbuf", "bfloat16", x=TRX + 256, q=256, qrep=4096, d=8192, xg=1024, ad=[32, 16, 16], lm=[16, 128], wem=[16, 128], bm=[16, 128],
-     ci=256, c2=256, resn=256, resx=256, nt=256, qg=1024, dg=1040, adg=[4, 16, 16], rs0=64, rs1=64, rs2=64, rr0=64, rr1=64, rr2=64)
-_pack("bfloat16", id=128, nid=128, bo=128, nbo=128, ntri=128, id14=128, sw=128, swd=128, sg=128, one=128, tmpb=128, ef=256, it=256,
-      dm=256, trib=256, resa=256, wm=512, e=256, fw=256, gw=256, c=256, jb=16, rj=16, zz=16, okt=32, h=16, f0=16, un=16, hj=16, cs=32,
+     ci=256, resn=256, resx=256, nt=256, qg=1024, dg=1040, adg=[4, 16, 16], rs0=64, rs1=64, rs2=64, rr0=64, rr1=64, rr2=64)
+_pack("bfloat16", id=128, nid=128, bo=128, nbo=128, ntri=128, id14=128, sw=128, swd=128, sg=128, one=128, ef=256, it=256,
+      dm=256, trib=256, resa=256, e=256, fw=256, gw=256, c=256, jb=16, rj=16, zz=16, okt=32, h=16, f0=16, un=16, hj=16, cs=32,
       ewa=32, ewb=32, xk=16, cap=64, qb=64, rz=64, got=16)
 _add("sbuf", "float16", moh=[16, 2], mo8=[16, 32], e8=128, pcg=64)
-_pack("float16", lic=512, ns=512, pl=32, u1h=16)
+_pack("float16", lic=512, ns=512, pl=16, u1h=16)
 _add("sbuf", "float32", pt=V + 256, m256=V, pf=1, sc=512, sw2=512, sg2=64, ym2=V, mt=256)
-_pack("float32", pm=1, pg=1, pidx=1, widx=1, evc=1, th32=1, th2k=1, dcol=16, idf=128, j2=16, trx=16, trp=32, ios=64, dmo=16, uf=32,
-      t16=16, dl=16, d1=16, d0=16, capf=64, wd=512, kw=512, plf=16, numf=16, nrb=256, cnt=256, l0=16, lt=16, xo=16, nl=512, um=64,
-      us=64, du=32, vf=32, pz=32, po=32, ms=256)
+_pack("float32", dv=512, numc=16, pm=1, pg=1, pidx=1, widx=1, evc=1, th32=1, th2k=1, dcol=16, idf=128, j2=16, trx=16, trp=32, ios=64,
+      dmo=16, uf=32, t16=16, dl=16, d1=16, d0=16, capf=64, wd=512, plf=16, numf=16, nrb=256, cnt=256, l0=16, lt=16, xo=16, nl=512,
+      um=64, us=64, du=32, pz=32, po=32, ms=256)
 _add("psum", "float32", b0=512, b1=512, b2=512, b3=512, b4=[16, 32], b5=512, b6=512, b7=512)
 SEMAPHORES = ["sv", "sa", "st", "sg", "loc"] + ["dma%d" % i for i in range(16)] + ["rq%d" % t for t in range(3)] + ["rp%d" % t for t in range(3)]
 
@@ -242,7 +242,6 @@ def rank_program(g, core, T, topo):
     fill(B("one"), 1.0)
     op("g", lambda: g.affine_select(B("id")[0], B("one")[0], [[-1, 128]], A.is_equal, 0.0, 0, 1), B("id"), B("one"))
     iota(B("ci"), [[0, 16], [1, 16]], 1)
-    iota(B("c2"), [[0, 16], [-2, 16]], -2)
     iota(B("ios"), [[1, 64]])
     ts(B("pmi"), B("pc"), 15, AND)
     ts(B("pgi"), B("pc"), 4, SHR)
@@ -264,7 +263,13 @@ def rank_program(g, core, T, topo):
     for s in range(2):
         ts(B("trp", (16 * s, 16 * s + 16)), B("j2"), float(TRP), A.add)
     ts(B("j2"), B("j2"), 2.0, A.mult)
-    ts(B("nid"), e128, B("pf"), A.is_equal, -1.0, A.mult)
+    ac(B("nid"), B("id"), AF.Copy, scale=-1.0)
+    ac(B("nbo"), B("bo"), AF.Copy, scale=-1.0)
+    op("g", lambda: g.affine_select(B("ntri")[0], B("nbo")[0], [[1, 128]], A.is_gt, 0.0, 0, -1), B("ntri"), B("nbo"))
+    ac(B("id14"), B("id"), AF.Copy, scale=1424.0)
+    ac(B("idf"), B("id"), AF.Copy)
+    ts(B("resx"), B("it"), 0.5, A.is_lt, -BIG - 2.0, A.mult)
+    ts(B("resx"), B("resx"), 2.0, A.add)
     fill(B("x", (0, PAD)), 0.0)
     fill(B("x", (PAD + H, TRX)), 0.0)
 
@@ -276,21 +281,23 @@ def rank_program(g, core, T, topo):
         for i in range(16 - QA, 16):
             ac(B("qrep", (i, 4096, 16)), B("q"), AF.Copy)
 
+    par = B("b1", (256, 272))
+
     def parity(last):
         for m in range(16):
-            mm(B("b6", (0, 16)), B("wem", m), B("q", (m, 256, 16)), m == 0, last and m == 15)
+            mm(par, B("wem", m), B("q", (m, 256, 16)), m == 0, last and m == 15)
 
     qrep_v(0, 5)
     ts(B("wem"), B("lm"), B("evc"), A.mult)
     parity(True)
+    op("v", lambda: vec.tensor_copy(T.z_mo8[0:8, :, :], T.z_moi[0:8, :]), B("mo8"), B("moi"))
+    op("v", lambda: vec.tensor_scalar(T.z_e8[0:8, :], T.z_nt[0:8, 0:128], T.z_pf[0:8, 0:1], None, A.is_equal), B("e8"), B("nt"), B("pf"))
+    op("t", lambda: pe.matmul(B("b4")[0], T.z_e8[0:8, :], T.z_mo8[0:8, :, :], True, True), B("b4"), B("e8"), B("mo8"))
     qrep_s()
     qrep_v(5, 16 - QA)
     cp(B("pt", (0, V)), B("pti"))
 
     def first_mothers():
-        op("v", lambda: vec.tensor_copy(T.z_mo8[0:8, :, :], T.z_moi[0:8, :]), B("mo8"), B("moi"))
-        op("v", lambda: vec.tensor_scalar(T.z_e8[0:8, :], T.z_nt[0:8, 0:128], T.z_pf[0:8, 0:1], None, A.is_equal), B("e8"), B("nt"), B("pf"))
-        op("t", lambda: pe.matmul(B("b4")[0], T.z_e8[0:8, :], T.z_mo8[0:8, :, :], True, True), B("b4"), B("e8"), B("mo8"))
         ts(B("dm"), B("it"), B("pm"), A.is_equal)
         ts(B("resa"), B("it"), 0.5, A.is_gt)
         for s in range(2):
@@ -301,13 +308,8 @@ def rank_program(g, core, T, topo):
 
     def late_constants():
         ts(B("dcol"), B("ef", (0, 16)), B("pm"), A.is_equal)
-        ts(B("resx"), B("resn"), -1.0, A.mult)
         ts(B("th32"), B("thi"), 32.0, A.mult)
         ts(B("th2k"), B("thi"), 2048.0, A.mult)
-        ts(B("nbo"), B("bo"), -1.0, A.mult)
-        ts(B("tmpb"), i128, B("pm"), A.is_gt, -1.0, A.mult)
-        tt(B("ntri"), B("tmpb"), B("bo"), A.mult)
-        ts(B("id14"), B("id"), 1424.0, A.mult)
         ts(B("t16", (0, 1)), B("podd"), -2.0, A.mult, 1.0, A.add)
         tt(B("t16", (0, 1)), B("t16", (0, 1)), B("pf"), A.add)
         ts(B("sw"), e128, B("t16", (0, 1)), A.is_equal)
@@ -325,7 +327,6 @@ def rank_program(g, core, T, topo):
         fill(B("dg", (0, 16)), -512.0)
         fill(B("fw", (64, 256)), 0.0)
         fill(B("gw", (64, 256)), 0.0)
-        cp(B("idf"), B("id"))
 
     xwin = B("x", (PAD, TRX))
     u0, u1 = B("uf", (0, 16)), B("uf", (16, 32))
@@ -357,7 +358,7 @@ def rank_program(g, core, T, topo):
             for m in range(16):
                 mm(out, B("lm", m), B("ad", (4 * k, 4 * k + 4), m), False, m == 15)
 
-        cp(B("bi"), B("b6", (0, 16)))
+        cp(B("bi"), par)
         ts(B("bq"), B("bi"), 1, AND)
         tt(u0, B("bq"), B("j2"), A.add)
 
@@ -376,7 +377,6 @@ def rank_program(g, core, T, topo):
         for a in range(2):
             mm(B("b%d" % (2 + a)), B("nid"), B("qrep", (512 * a, 512 * a + 512)), True, False)
             mm(B("b%d" % (2 + a)), B("id"), B("xg", (512 * a, 512 * a + 512)), False, True)
-            ac(B("ad", (2 * a, 2 * a + 2)), B("b%d" % (2 + a)), AF.Abs)
         diff(1)
         absd(1)
         if t == 0:
@@ -384,8 +384,10 @@ def rank_program(g, core, T, topo):
             second_town()
             cp(B("uu", (16, 32)), u1)
             gat(B("li", (256, 512)), B("pt", (0, V)), B("uu", (16, 32)))
-        reduce(0)
+        for a in range(2):
+            ac(B("ad", (2 * a, 2 * a + 2)), B("b%d" % (2 + a)), AF.Abs)
         reduce(1)
+        reduce(0)
         diff(2)
         if t == 0:
             ac(B("m256"), B("b4"), AF.Copy, scale=256.0)
@@ -399,9 +401,8 @@ def rank_program(g, core, T, topo):
         reduce(4)
         if t == 0:
             late_constants()
-        gat_tt(B("vv"), B("m256"), B("uu", (16, 32)), B("q"), A.add)
         tt(B("du"), B("uf"), B("trp"), A.subtract)
-        cp(B("u1h"), u1)
+        ac(B("u1h"), u1, AF.Copy)
         diff(5)
         absd(5)
         reduce(5)
@@ -418,9 +419,9 @@ def rank_program(g, core, T, topo):
             absd(7, (hf,))
         reduce(7)
         tt(B("xk"), B("b6", (64, 80)), B("f0"), A.mult)
+        tt(B("du", (0, 16)), B("du", (0, 16)), B("f0"), A.mult)
         tt(B("dl"), B("b6", (48, 64)), B("xk"), A.mult)
-        tt(B("kw", (0, 256)), k0, B("c2"), A.add)
-        scan(B("sw2", (0, 256)), B("resx"), B("kw", (0, 256)), A.min, A.max)
+        scan(B("sw2", (0, 256)), B("resx"), k0, A.add, A.max)
         tt(B("d1"), B("dl"), B("bq"), A.mult)
         tt(B("d0"), B("dl"), B("d1"), A.subtract)
         tt(B("moh", (0, 16), 1), B("moh", (0, 16), 1), B("d1"), A.add)
@@ -429,6 +430,7 @@ def rank_program(g, core, T, topo):
         ts(B("ke", (0, 16)), B("kc", (0, 16)), 31, AND)
         cp(B("ewa", (0, 16)), B("ke", (0, 16)))
         tt(B("dmo"), B("moh", (0, 16), 1), B("moh", (0, 16), 0), A.subtract)
+        gat_tt(B("vv"), B("m256"), B("uu", (16, 32)), B("q"), A.add)
         scan(B("sc", (256, 512)), B("resn"), k1, A.max, A.min)
         ts(B("okt", (16, 32)), best1, B("th32"), A.is_lt)
         tt(B("h"), B("okt", (0, 16)), B("okt", (16, 32)), A.max)
@@ -442,7 +444,7 @@ def rank_program(g, core, T, topo):
         ts(B("kc", (16, 32)), best1, B("th32"), A.min)
         ts(B("ke", (16, 32)), B("kc", (16, 32)), 31, AND)
         tt(B("ewa", (16, 32)), B("ke", (16, 32)), B("f0"), A.mult)
-        ts(B("un"), B("h"), -1.0, A.mult, 1.0, A.add)
+        ac(B("un"), B("h"), AF.Identity, bias=1.0, scale=-1.0)
         mm(B("b6", (32, 33)), B("bo"), B("cs", (16, 17)), True, True)
         cp(B("offu"), off)
         scat(B(pk, (0, 256)), B("offu"), B("vv"))
@@ -453,15 +455,13 @@ def rank_program(g, core, T, topo):
                 ac(B("bm", m), B("bo"), AF.Copy, scale=B("dcol", (m, m + 1)))
         for m in range(16):
             mm(B("b2", (m, 512, 16)), B("bm", m), B("ewa"), True, True)
-        tt(B("kw", (256, 512)), k1, B("c2"), A.add)
-        ts(B("plf"), off, 1.0 / 32, A.mult, (1216.0 + 64 * t) / 32, A.add)
-        for s in range(2):
-            tt(B("pl", (16 * s, 16 * s + 16)), B("plf"), B("un"), A.mult)
+        ac(B("plf"), off, AF.Identity, bias=(1216.0 + 64 * t) / 32, scale=1.0 / 32)
+        tt(B("pl"), B("plf"), B("un"), A.mult)
         ts(B("capf"), B("ios"), B("b6", (32, 33)), A.add, 256.0, A.is_lt)
-        ts(B("cap"), B("capf"), 256.0, A.mult, -1.0, A.add)
+        ac(B("cap"), B("capf"), AF.Identity, bias=-1.0, scale=256.0)
         ts(B("b3"), B("b2"), B("pidx"), A.is_equal)
         tt(B("ns"), B("b3"), B("lic"), A.mult)
-        scan(B("sw2", (256, 512)), B("resx"), B("kw", (256, 512)), A.min, A.max)
+        scan(B("sw2", (256, 512)), B("resx"), k1, A.add, A.max)
         ts(B("wi"), B("sw2", (15, 512, 16)), -64.0, A.max)
         ts(B("we"), B("wi"), 31, AND)
         cp(B("ewb"), B("we"))
@@ -471,31 +471,28 @@ def rank_program(g, core, T, topo):
                 mm(num, B("lm", m), B("ns", (256 * s + m, 256 * s + 256, 16)), m == 0 and s == 0, False)
         mm(num, B("id14"), B("h"), False, True)
         for m in range(16):
-            mm(B("b4", (0, 16), (2 * m, 2 * m + 2)), B("bm", m), B("moh"), True, True)
-        for m in range(16):
             mm(B("b7", (m, 512, 16)), B("bm", m), B("ewb"), True, True)
-        mm(B("b5"), B("nid"), B("lic"), True, False)
+        vp = B("b5", (0, 256))
         for s in range(2):
-            for s2 in range(2):
-                mm(B("b5", (256 * s, 256 * s + 256)), B("bo"), B("ns", (256 * s2, 256 * s2 + 256)), False, False)
+            mm(vp, B("bo"), B("ns", (256 * s, 256 * s + 256)), s == 0, False)
         for m in range(16):
-            mm(B("b5", (m, 512, 16)), B("bm", m), B("pl"), False, m == 15)
+            mm(B("b5", (m, 256, 16)), B("bm", m), B("pl"), False, m == 15)
         cp(B("numu"), num)
-        cp(B("numf"), num)
+        ac(B("numc"), num, AF.Identity, bias=-44.5, scale=1.0 / 32)
+        ac(B("numf"), num, AF.Copy)
         gat_tt(B("sh"), B("x", (0, TRX)), B("numu"), B("q"), A.add)
         ts(B("rn"), B("sh"), 1, SHR)
-        if not end:
-            ts(B("qh"), B("sh"), 255, AND)
         arrived(pkr, "rq%d" % t, came_from(guest), core)
+        ts(B("qi"), B(pkr), 255, AND)
+        cp(B("qb"), B("qi"))
+        for i in range(5, 16):
+            ac(B("qg", (i, 1024, 16)), B("qb"), AF.Copy)
         ts(B("u2i"), B(pkr), 8, SHR)
         tt(B("um"), B("u2i"), B("dm", (0, 64)), A.mult)
         scan(B("us"), B("resa", (0, 64)), B("um"), A.mult, A.add)
-        ts(B("qi"), B(pkr), 255, AND)
         cp(B("u2u"), B("us", (15, 64, 16)))
-        cp(B("qb"), B("qi"))
         gat(B("lig"), B("pt", (0, V)), B("u2u"))
-        for i in range(8):
-            ac(B("qg", (8 + i, 1024, 16)), B("qb"), AF.Copy)
+        for i in range(5):
             cp(B("qg", (i, 1024, 16)), B("qb"))
         for hf in range(2):
             gat_tt(B("dg", (16 + 512 * hf, 528 + 512 * hf)), xwin, B("lig", (32 * hf, 32 * hf + 32)), B("qg", (512 * hf, 512 * hf + 512)), A.subtract)
@@ -504,21 +501,19 @@ def rank_program(g, core, T, topo):
         mm(gk, B("id"), B("pcg"), True, False)
         for m in range(16):
             mm(gk, B("lm", m), B("adg", (0, 4), m), False, m == 15)
-        ts(B("wm"), B("b7"), B("widx"), A.is_equal)
-        tt(B("wd"), B("b5"), B("wm"), A.mult)
+        ts(B("b3"), B("b7"), B("widx"), A.is_equal)
+        for s in range(2):
+            tt(B("dv", (256 * s, 256 * s + 256)), vp, B("lic", (256 * s, 256 * s + 256)), A.subtract)
+        tt(B("wd"), B("b3"), B("dv"), A.mult)
+        tt(B("nrb"), vp, B("trib"), A.add)
         scan(B("sg2"), B("resn", (0, 64)), gk, A.max, A.min)
         ts(B("gkc"), B("sg2", (15, 64, 16)), B("th2k"), A.min)
         ts(B("gpos"), B("gkc"), 2047, AND)
         cp(B("posu"), B("gpos"))
         gat_tt(B(rs), B("dg"), B("posu"), B("qb"), A.add)
         send(guest, rs, "rp%d" % t, (rr, 64))
-        nr = B("b2", (0, 256))
-        mm(nr, B("id"), B("trib"), True, False)
-        for s in range(2):
-            mm(nr, B("bo"), B("ns", (256 * s, 256 * s + 256)), False, False)
         for m in range(16):
-            mm(B("b2", (m, 256, 16)), B("bm", m), B("pl", (0, 16)), False, m == 15)
-        ac(B("nrb"), nr, AF.Identity, bias=1424.0, scale=32.0)
+            mm(B("b4", (0, 16), (2 * m, 2 * m + 2)), B("bm", m), B("moh"), True, True)
         mm(B("b7"), B("id"), B("lic"), True, False)
         mm(B("b7"), B("idf"), B("wd"), False, True)
         if not end:
@@ -527,7 +522,7 @@ def rank_program(g, core, T, topo):
             ac(B("ym2"), B("b4"), AF.Copy)
             dma("y", T.ym[:], T.z_ym2[0:128:16, :], (B("ym2"),), ())
         ac(B("nl"), B("b7"), AF.Identity, bias=1408.0, scale=32.0)
-        gat_tt(B("e"), B("numf"), B("expl"), B("nrb"), A.is_equal)
+        gat_tt(B("e"), B("numc"), B("expl"), B("nrb"), A.is_equal)
         scan(B("cnt"), B("resa"), B("e"), A.mult, A.add)
         ts(B("l0"), B("cnt", (15, 256, 16)), 0.5, A.is_ge)
         tt(B("l0"), B("l0"), B("un"), A.max)
@@ -548,7 +543,7 @@ def rank_program(g, core, T, topo):
         for m in range(16):
             mm(came, B("lm", m), B("c", (m, 256, 16)), m == 0, m == 15)
         if not end:
-            gat_tt(B("s1"), B("gw"), B("offu"), B("qh"), A.add)
+            gat_tt(B("s1"), B("gw"), B("offu"), B("sh"), A.add)
             ts(B("s2"), B("s1"), 255, AND)
             cp(B("q"), B("s2"))
             parity(False)
@@ -556,11 +551,10 @@ def rank_program(g, core, T, topo):
             qrep_v(0, 16 - QA)
         ac(gcol, B("gw", (0, 64)), AF.Copy)
         tt(B("got"), B("h"), came, A.max)
-        cp(B("vf", (16, 32)), came)
         if not end:
-            mm(B("b6", (0, 16)), B("sg"), B("got"), False, True)
-        tt(B("vf", (0, 16)), B("got"), B("f0"), A.mult)
-        tt(B("pz"), B("vf"), B("du"), A.mult)
+            mm(par, B("sg"), B("got"), False, True)
+        tt(B("pz", (0, 16)), B("got"), B("du", (0, 16)), A.mult)
+        tt(B("pz", (16, 32)), came, B("du", (16, 32)), A.mult)
         tt(B("po"), B("pz"), B("trp"), A.add)
         cp(B("poff"), B("po"))
         scat(B("pt"), B("poff", (16, 32)), B("nl", (256, 512)))

import numpy as np
from concourse.mybir import AluOpType as A, ActivationFunctionType as AF

R_, H, V, K, CAP, N = 3, 2624, 512, 256, 64, 8
PAD, W = 16, 2816
TRX, TRP = PAD + W, V
BIG = float(2 ** 30)
ENG = 8
QA = 10

BUF, AT = {}, {}
SCRATCH = {}


def _add(where, dtype, **kw):
    for k, v in kw.items():
        BUF[k] = (where, [128] + (v if isinstance(v, list) else [v]), dtype)
        SCRATCH["z_" + k] = BUF[k]


def _pack(dtype, **kw):
    at = 0
    for k, v in kw.items():
        BUF[k] = ("sbuf", [128, v], dtype)
        AT[k] = ("t_" + dtype, at, v)
        at += (v + 15) // 16 * 16
    SCRATCH["t_" + dtype] = ("sbuf", [128, at], dtype)


_add("sbuf", "int32", pti=V, moi=V, thi=1, vv=256, pk0=256, pk1=256, pk2=256, pkr0=64, pkr1=64, pkr2=64, sh=256, rn=256,
     s1=256, s2=256)
_pack("int32", pc=1, pmi=1, pgi=1, podd=1, bi=16, bq=16, kc=32, ke=32, wi=32, we=32, u2i=64, qi=64, gkc=4, gpos=4)
_add("sbuf", "uint16", li=512)
_pack("uint16", uu=32, offu=16, numu=16, xoff=32, poff=32, u2u=4, posu=4, lig=64, expl=16)
_add("sbuf", "bfloat16", x=TRX + 256, q=256, qrep=4096, d=8192, xg=1024, ad=[32, 16, 16], lm=[16, 128], wem=[16, 128], bm=[16, 128],
     ci=256, resn=256, resx=256, nt=256, qg=1024, dg=1040, adg=[4, 16, 16], rs0=64, rs1=64, rs2=64, rr0=64, rr1=64, rr2=64)
_pack("bfloat16", id=128, nid=128, bo=128, nbo=128, ntri=128, id14=128, sw=128, swd=128, sg=128, one=128, ef=256, it=256,
      dm=256, trib=256, resa=256, e=256, fw=256, gw=256, c=256, jb=16, rj=16, zz=16, okt=32, h=16, f0=16, un=16, hj=16, cs=32,
      ewa=32, ewb=32, xk=16, cap=64, qb=64, rz=64, got=16)
_add("sbuf", "float16", moh=[16, 2], mo8=[16, 32], e8=128, pcg=64)
_pack("float16", lic=512, ns=512, pl=16, u1h=16)
_add("sbuf", "float32", pt=V + 256, m256=V, pf=1, sc=512, sw2=512, sg2=64, ym2=V, mt=256)
_pack("float32", dv=512, numc=16, pm=1, pg=1, pidx=1, widx=1, evc=1, th32=1, th2k=1, dcol=16, idf=128, j2=16, trx=16, trp=32, ios=64,
      dmo=16, uf=32, t16=16, dl=16, d1=16, d0=16, capf=64, wd=512, plf=16, numf=16, nrb=256, cnt=256, l0=16, lt=16, xo=16, nl=512,
      um=64, us=64, du=32, pz=32, po=32, ms=256)
_add("psum", "float32", b0=512, b1=512, b2=512, b3=512, b4=[16, 32], b5=512, b6=512, b7=512)
SEMAPHORES = ["sv", "sa", "st", "sg", "loc"] + ["dma%d" % i for i in range(16)] + ["rq%d" % t for t in range(3)] + ["rp%d" % t for t in range(3)]


def _emask(topo, src, dst, n):
    m = 0
    for e in topo.engines(src, dst)[:n]:
        m |= 1 << e
    return m


def _relay(topo, src, dst):
    if topo.may_write(src, dst):
        return None
    for c in topo.cores_of(src):
        if topo.die(c) == topo.die(src) and topo.may_write(c, dst):
            return c
    return None


def _send(g, T, topo, src, dst, name, sem, cols=None):
    rid, pid = topo.addr(dst, src)
    ap_out = T["z_" + name][:] if cols is None else T["z_" + cols[0]][:]
    ap_in = T["z_" + name][:] if cols is None else T["z_" + name][:, 0:cols[1]]
    g.remote_dma(ap_out, ap_in, T.sem[sem], T.sem.loc, pid, rid, _emask(topo, src, dst, ENG))
    return len(topo.engines(src, dst)[:ENG])


def _hand_on(g, core, T, topo):
    n = 0
    for t in range(R_):
        for kind in ("rq", "rp"):
            for r in range(N):
                a, b = T.cores[r], T.cores[(r + 1 + t) % N]
                src, dst = (a, b) if kind == "rq" else (b, a)
                if _relay(topo, src, dst) == core:
                    g.wait_ge(T.sem["%s%d" % (kind, t)], len(topo.engines(src, core)[:ENG]))
                    n += _send(g, T, topo, core, dst, ("pkr%d" if kind == "rq" else "rr%d") % t, "%s%d" % (kind, t))
    if n:
        g.wait_ge(T.sem.loc, n)


def rank_program(g, core, T, topo):
    rank = T.rank_of(core)
    if rank is None:
        _hand_on(g, core, T, topo)
        return

    Q = {"v": g.vector, "s": g.scalar, "t": g.tensor, "g": g, "y": g.sync}
    SEM = {"v": "sv", "s": "sa", "t": "st", "g": "sg"}
    total, hist, clk, known, cache = {}, {}, {}, {k: {} for k in "vstgy"}, {}
    ndma = [0]

    def B(name, *idx):
        key = (name, idx)
        if key not in cache:
            full = (slice(None),) + tuple(slice(*i) if isinstance(i, tuple) else i for i in idx)
            m = np.zeros(BUF[name][1][1:], bool)
            m[tuple(full[1:])] = True
            if name in AT:
                phys, at, w = AT[name]
                lo, hi, st = (tuple(idx[0]) + (1,))[:3] if idx else (0, w, 1)
                ap = T[phys][:, at + lo:at + hi:st] if st > 1 else T[phys][:, at + lo:at + hi]
            else:
                ap = T["z_" + name][full]
            cache[key] = (ap, name, int.from_bytes(np.packbits(m.ravel(), bitorder="little").tobytes(), "little"))
        return cache[key]

    def deps(q, reads, writes):
        need = {}

        def want(rec):
            need[rec[2]] = max(need.get(rec[2], 0), rec[3])
        for wr, lst in ((False, reads), (True, writes)):
            for ap, name, m in lst:
                ps = BUF[name][0] == "psum"
                for rec in hist.get(name, ()):
                    same = rec[4] == q
                    if ps and not same:
                        want(rec)
                    elif rec[0] & m:
                        if rec[1] and not (ps and q == "t" and same):
                            want(rec)
                        elif wr and not rec[1] and not same:
                            want(rec)
        return need

    def wait(q, need):
        kn = known[q]
        todo = {s: v for s, v in need.items() if kn.get(s, 0) < v}
        for s, v in todo.items():
            if any(o != s and clk[(o, w)].get(s, 0) >= v for o, w in todo.items()):
                continue
            if kn.get(s, 0) >= v:
                continue
            Q[q].wait_ge(T.sem[s], v)
            for k2, v2 in clk[(s, v)].items():
                kn[k2] = max(kn.get(k2, 0), v2)
            kn[s] = max(kn.get(s, 0), v)

    def record(q, reads, writes, sem, val):
        clk[(sem, val)] = dict(known[q])
        for ap, name, m in writes:
            hist[name] = [r for r in hist.get(name, []) if r[0] & ~m] + [(m, True, sem, val, q)]
        for ap, name, m in reads:
            hist[name] = [r for r in hist.get(name, []) if r[1] or r[4] != q or r[0] & ~m] + [(m, False, sem, val, q)]

    def op(q, fn, out, *ins):
        wait(q, deps(q, ins, (out,)))
        sem = SEM[q]
        total[sem] = total.get(sem, 0) + 1
        fn().then_inc(T.sem[sem], 1)
        record(q, ins, (out,), sem, total[sem])

    def dma(q, out, in_, reads, writes):
        wait(q, deps(q, reads, writes))
        sem = "dma%d" % ndma[0]
        ndma[0] += 1
        total[sem] = 16
        Q[q].dma_start(out, in_).then_inc(T.sem[sem], 16)
        record(q, reads, writes, sem, 16)

    def arrived(name, sem, src, dst):
        n = len(topo.engines(src, dst)[:ENG])
        total[sem] = n
        clk[(sem, n)] = {}
        hist[name] = [((1 << 64) - 1, True, sem, n, "r")]

    vec, act, pe = g.vector, g.scalar, g.tensor

    def cp(out, in_):
        op("v", lambda: vec.tensor_copy(out[0], in_[0]), out, in_)

    def tt(out, a, b, o):
        op("v", lambda: vec.tensor_tensor(out[0], a[0], b[0], o), out, a, b)

    def ts(out, a, s1, o1, s2=None, o2=None):
        cols = [s for s in (s1, s2) if isinstance(s, tuple)]
        x1 = s1[0] if isinstance(s1, tuple) else s1
        x2 = s2[0] if isinstance(s2, tuple) else s2
        if o2 is None:
            op("v", lambda: vec.tensor_scalar(out[0], a[0], x1, None, o1), out, a, *cols)
        else:
            op("v", lambda: vec.tensor_scalar(out[0], a[0], x1, x2, o1, o2), out, a, *cols)

    def scan(out, d0, d1, o1, o2):
        op("v", lambda: vec.tensor_tensor_scan(out[0], d0[0], d1[0], 0.0, o1, o2), out, d0, d1)

    def gat(out, win, off):
        op("v", lambda: vec.tensor_copy(out[0], win[0].indirect(off[0])), out, win, off)

    def gat_tt(out, win, off, b, o):
        op("v", lambda: vec.tensor_tensor(out[0], win[0].indirect(off[0]), b[0], o), out, win, off, b)

    def scat(win, off, in_):
        op("v", lambda: vec.tensor_copy(win[0].indirect(off[0]), in_[0]), win, off, in_)

    def fill(out, c):
        op("v", lambda: vec.memset(out[0], c), out)

    def ac(out, in_, f, bias=0.0, scale=1.0):
        if isinstance(scale, tuple):
            op("s", lambda: act.activation(out[0], in_[0], f, bias=bias, scale=scale[0]), out, in_, scale)
        else:
            op("s", lambda: act.activation(out[0], in_[0], f, bias=bias, scale=scale), out, in_)

    def agat(out, win, off, bias=0.0, scale=1.0):
        op("s", lambda: act.activation(out[0], win[0].indirect(off[0]), AF.Identity, bias=bias, scale=scale), out, win, off)

    def mm(out, l, r, start, stop):
        op("t", lambda: pe.matmul(out[0], l[0], r[0], start, stop), out, l, r)

    def iota(out, pattern, base=0, mult=0):
        if BUF[out[1]][2] == "int32":
            op("g", lambda: g.iota(out[0], pattern, base, mult), out)
        else:
            op("g", lambda: g.iota(out[0], pattern, base, mult, allow_small_or_imprecise_dtypes=True), out)

    def send(dst, name, sem, cols=None):
        hop = _relay(topo, core, dst)
        src = B(name) if cols is None else B(name, (0, cols[1]))
        wait("g", deps("g", (src,), ()))
        n = _send(g, T, topo, core, dst if hop is None else hop, name, sem, cols)
        total["loc"] = total.get("loc", 0) + n

    dma("y", B("q")[0], T.qs[:], (), (B("q"),))
    dma("s", B("x", (PAD, PAD + H))[0], T.x[:], (), (B("x", (PAD, PAD + H)),))
    dma("y", B("pti")[0], T.towns[:], (), (B("pti"),))
    dma("y", T.z_moi[0:8, :], T.mo[:], (), (B("moi"),))
    dma("y", B("thi")[0], T.th[:], (), (B("thi"),))
    AND, SHR = A.bitwise_and, A.arith_shift_right
    iota(B("pc"), [[1, 1]], 0, 1)
    iota(B("nt"), [[1, 16], [0, 16]])
    iota(B("it"), [[0, 16], [1, 16]])
    iota(B("ef"), [[1, 256]])
    fill(B("lm"), 0.0)
    fill(B("one"), 1.0)
    op("g", lambda: g.affine_select(B("id")[0], B("one")[0], [[-1, 128]], A.is_equal, 0.0, 0, 1), B("id"), B("one"))
    iota(B("ci"), [[0, 16], [1, 16]], 1)
    iota(B("ios"), [[1, 64]])
    ts(B("pmi"), B("pc"), 15, AND)
    ts(B("pgi"), B("pc"), 4, SHR)
    ts(B("podd"), B("pc"), 1, AND)
    cp(B("pg"), B("pgi"))
    ts(B("evc"), B("podd"), -1.0 / 32, A.mult, 1.0 / 32, A.add)
    cp(B("pm"), B("pmi"))
    cp(B("pf"), B("pc"))
    e128, i128, n128 = B("ef", (0, 128)), B("it", (0, 128)), B("nt", (0, 128))
    ts(B("bo"), n128, B("pg"), A.is_equal)
    for m in range(16):
        ac(B("lm", m, (m, 128, 16)), B("bo", (m, 128, 16)), AF.Copy, scale=32.0)
    ts(B("resn"), B("it"), 0.5, A.is_lt, 2 * BIG, A.mult)
    ts(B("resn"), B("resn"), -BIG, A.add)
    ts(B("j2"), B("ef", (0, 16)), 16.0, A.mult, B("pm"), A.add)
    cp(B("jb"), B("j2"))
    ts(B("rj"), B("j2"), -1.0, A.mult, 255.0, A.add)
    ts(B("trx"), B("j2"), float(TRX), A.add)
    for s in range(2):
        ts(B("trp", (16 * s, 16 * s + 16)), B("j2"), float(TRP), A.add)
    ts(B("j2"), B("j2"), 2.0, A.mult)
    ac(B("nid"), B("id"), AF.Copy, scale=-1.0)
    ac(B("nbo"), B("bo"), AF.Copy, scale=-1.0)
    op("g", lambda: g.affine_select(B("ntri")[0], B("nbo")[0], [[1, 128]], A.is_gt, 0.0, 0, -1), B("ntri"), B("nbo"))
    ac(B("id14"), B("id"), AF.Copy, scale=1424.0)
    ac(B("idf"), B("id"), AF.Copy)
    ts(B("resx"), B("it"), 0.5, A.is_lt, -BIG - 2.0, A.mult)
    ts(B("resx"), B("resx"), 2.0, A.add)
    fill(B("x", (0, PAD)), 0.0)
    fill(B("x", (PAD + H, TRX)), 0.0)

    def qrep_v(lo, hi):
        for i in range(lo, hi):
            cp(B("qrep", (i, 4096, 16)), B("q"))

    def qrep_s():
        for i in range(16 - QA, 16):
            ac(B("qrep", (i, 4096, 16)), B("q"), AF.Copy)

    par = B("b1", (256, 272))

    def parity(last):
        for m in range(16):
            mm(par, B("wem", m), B("q", (m, 256, 16)), m == 0, last and m == 15)

    qrep_v(0, 5)
    ts(B("wem"), B("lm"), B("evc"), A.mult)
    parity(True)
    op("v", lambda: vec.tensor_copy(T.z_mo8[0:8, :, :], T.z_moi[0:8, :]), B("mo8"), B("moi"))
    op("v", lambda: vec.tensor_scalar(T.z_e8[0:8, :], T.z_nt[0:8, 0:128], T.z_pf[0:8, 0:1], None, A.is_equal), B("e8"), B("nt"), B("pf"))
    op("t", lambda: pe.matmul(B("b4")[0], T.z_e8[0:8, :], T.z_mo8[0:8, :, :], True, True), B("b4"), B("e8"), B("mo8"))
    qrep_s()
    qrep_v(5, 16 - QA)
    cp(B("pt", (0, V)), B("pti"))

    def first_mothers():
        ts(B("dm"), B("it"), B("pm"), A.is_equal)
        ts(B("resa"), B("it"), 0.5, A.is_gt)
        for s in range(2):
            tt(B("mt"), B("b4", (0, 16), (s, 32, 2)), B("dm"), A.mult)
            scan(B("ms"), B("resa"), B("mt"), A.mult, A.add)
            cp(B("moh", (0, 16), s), B("ms", (15, 256, 16)))
        tt(B("dmo"), B("moh", (0, 16), 1), B("moh", (0, 16), 0), A.subtract)

    def late_constants():
        ts(B("dcol"), B("ef", (0, 16)), B("pm"), A.is_equal)
        ts(B("th32"), B("thi"), 32.0, A.mult)
        ts(B("th2k"), B("thi"), 2048.0, A.mult)
        ts(B("t16", (0, 1)), B("podd"), -2.0, A.mult, 1.0, A.add)
        tt(B("t16", (0, 1)), B("t16", (0, 1)), B("pf"), A.add)
        ts(B("sw"), e128, B("t16", (0, 1)), A.is_equal)
        tt(B("swd"), B("sw"), B("id"), A.subtract)
        ts(B("sg"), i128, B("pm"), A.is_equal)
        fill(B("zz"), 0.0)
        fill(B("cs"), 0.0)
        ts(B("trib"), B("it"), B("pm"), A.is_ge, 1024.0, A.mult)
        ts(B("pidx"), B("pm"), 1.0, A.add)
        ts(B("widx"), B("pm"), -1.0, A.mult, 31.0, A.add)
        cp(B("expl"), B("ios", (0, 16)))
        ts(B("t16", (0, 1)), B("pm"), 16.0, A.mult, 16.0, A.add)
        ts(B("um"), B("nt", (0, 64)), 256.0, A.mult, B("t16", (0, 1)), A.add)
        tt(B("pcg"), B("um"), B("it", (0, 64)), A.add)
        fill(B("dg", (0, 16)), -512.0)
        fill(B("fw", (64, 256)), 0.0)
        fill(B("gw", (64, 256)), 0.0)

    xwin = B("x", (PAD, TRX))
    u0, u1 = B("uf", (0, 16)), B("uf", (16, 32))
    k0, k1 = B("b0", (0, 256)), B("b1", (0, 256))
    best0, best1 = B("sc", (15, 256, 16)), B("sc", (271, 512, 16))

    for t in range(R_):
        end = t == R_ - 1
        guest, host_of = T.cores[(rank - 1 - t) % N], T.cores[(rank + 1 + t) % N]
        pk, pkr, rs, rr = "pk%d" % t, "pkr%d" % t, "rs%d" % t, "rr%d" % t

        def came_from(src):
            hop = _relay(topo, src, core)
            return src if hop is None else hop

        def diff(k, parts=(0, 1)):
            lo, hi = 2 * k + parts[0], 2 * k + parts[-1] + 1
            r = lo % 8
            gat_tt(B("d", (512 * lo, 512 * hi)), xwin, B("li", (32 * lo, 32 * hi)), B("qrep", (512 * r, 512 * (r + hi - lo))), A.subtract)

        def absd(k, parts=(0, 1)):
            lo, hi = 2 * k + parts[0], 2 * k + parts[-1] + 1
            ac(B("ad", (2 * lo, 2 * hi)), B("d", (512 * lo, 512 * hi)), AF.Abs)

        def reduce(k):
            s, c = k // 4, k % 4
            out = B("b%d" % s, (64 * c, 64 * c + 64))
            mm(out, B("id"), B("ci", (64 * c, 64 * c + 64)), True, False)
            for m in range(16):
                mm(out, B("lm", m), B("ad", (4 * k, 4 * k + 4), m), False, m == 15)

        cp(B("bi"), par)
        ts(B("bq"), B("bi"), 1, AND)
        tt(u0, B("bq"), B("j2"), A.add)

        def second_town():
            tt(B("t16"), B("bq"), B("dmo"), A.mult)
            tt(u1, B("t16"), B("moh", (0, 16), 0), A.add)

        if t == 0:
            cp(B("uu", (0, 16)), u0)
            gat(B("li", (0, 256)), B("pt", (0, V)), B("uu", (0, 16)))
        else:
            second_town()
            cp(B("uu"), B("uf"))
            gat(B("li"), B("pt", (0, V)), B("uu"))
        agat(B("xg"), xwin, B("li", (0, 64)))
        for a in range(2):
            mm(B("b%d" % (2 + a)), B("nid"), B("qrep", (512 * a, 512 * a + 512)), True, False)
            mm(B("b%d" % (2 + a)), B("id"), B("xg", (512 * a, 512 * a + 512)), False, True)
        diff(1)
        absd(1)
        if t == 0:
            first_mothers()
            second_town()
            cp(B("uu", (16, 32)), u1)
            gat(B("li", (256, 512)), B("pt", (0, V)), B("uu", (16, 32)))
        for a in range(2):
            ac(B("ad", (2 * a, 2 * a + 2)), B("b%d" % (2 + a)), AF.Abs)
        reduce(1)
        reduce(0)
        diff(2)
        if t == 0:
            ac(B("m256"), B("b4"), AF.Copy, scale=256.0)
        absd(2)
        reduce(2)
        diff(3)
        absd(3)
        reduce(3)
        diff(4)
        absd(4)
        reduce(4)
        if t == 0:
            late_constants()
        tt(B("du"), B("uf"), B("trp"), A.subtract)
        ac(B("u1h"), u1, AF.Copy)
        diff(5)
        absd(5)
        reduce(5)
        scan(B("sc", (0, 256)), B("resn"), k0, A.max, A.min)
        ts(B("okt", (0, 16)), best0, B("th32"), A.is_lt)
        ts(B("f0"), B("okt", (0, 16)), -1.0, A.mult, 1.0, A.add)
        diff(6)
        absd(6)
        mm(B("b6", (48, 64)), B("swd"), B("u1h"), True, True)
        mm(B("b6", (64, 80)), B("sw"), B("f0"), True, True)
        reduce(6)
        for hf in range(2):
            diff(7, (hf,))
            absd(7, (hf,))
        reduce(7)
        tt(B("xk"), B("b6", (64, 80)), B("f0"), A.mult)
        tt(B("du", (0, 16)), B("du", (0, 16)), B("f0"), A.mult)
        tt(B("dl"), B("b6", (48, 64)), B("xk"), A.mult)
        scan(B("sw2", (0, 256)), B("resx"), k0, A.add, A.max)
        tt(B("d1"), B("dl"), B("bq"), A.mult)
        tt(B("d0"), B("dl"), B("d1"), A.subtract)
        tt(B("moh", (0, 16), 1), B("moh", (0, 16), 1), B("d1"), A.add)
        tt(B("moh", (0, 16), 0), B("moh", (0, 16), 0), B("d0"), A.add)
        ts(B("kc", (0, 16)), best0, B("th32"), A.min)
        ts(B("ke", (0, 16)), B("kc", (0, 16)), 31, AND)
        cp(B("ewa", (0, 16)), B("ke", (0, 16)))
        tt(B("dmo"), B("moh", (0, 16), 1), B("moh", (0, 16), 0), A.subtract)
        gat_tt(B("vv"), B("m256"), B("uu", (16, 32)), B("q"), A.add)
        scan(B("sc", (256, 512)), B("resn"), k1, A.max, A.min)
        ts(B("okt", (16, 32)), best1, B("th32"), A.is_lt)
        tt(B("h"), B("okt", (0, 16)), B("okt", (16, 32)), A.max)
        scan(B("cs", (1, 17)), B("h"), B("zz"), A.add, A.add)
        tt(B("hj"), B("h"), B("rj"), A.mult)
        off = B("b6", (16, 32))
        mm(off, B("id"), B("jb"), True, False)
        mm(off, B("ntri"), B("h"), False, False)
        mm(off, B("nbo"), B("cs", (0, 16)), False, False)
        mm(off, B("id"), B("hj"), False, True)
        ts(B("kc", (16, 32)), best1, B("th32"), A.min)
        ts(B("ke", (16, 32)), B("kc", (16, 32)), 31, AND)
        tt(B("ewa", (16, 32)), B("ke", (16, 32)), B("f0"), A.mult)
        ac(B("un"), B("h"), AF.Identity, bias=1.0, scale=-1.0)
        mm(B("b6", (32, 33)), B("bo"), B("cs", (16, 17)), True, True)
        cp(B("offu"), off)
        scat(B(pk, (0, 256)), B("offu"), B("vv"))
        send(host_of, pk, "rq%d" % t, (pkr, 64))
        agat(B("lic"), B("pt", (0, V)), B("uu"), bias=-44.0, scale=1.0 / 32)
        if t == 0:
            for m in range(16):
                ac(B("bm", m), B("bo"), AF.Copy, scale=B("dcol", (m, m + 1)))
        for m in range(16):
            mm(B("b2", (m, 512, 16)), B("bm", m), B("ewa"), True, True)
        ac(B("plf"), off, AF.Identity, bias=(1216.0 + 64 * t) / 32, scale=1.0 / 32)
        tt(B("pl"), B("plf"), B("un"), A.mult)
        ts(B("capf"), B("ios"), B("b6", (32, 33)), A.add, 256.0, A.is_lt)
        ac(B("cap"), B("capf"), AF.Identity, bias=-1.0, scale=256.0)
        ts(B("b3"), B("b2"), B("pidx"), A.is_equal)
        tt(B("ns"), B("b3"), B("lic"), A.mult)
        scan(B("sw2", (256, 512)), B("resx"), k1, A.add, A.max)
        ts(B("wi"), B("sw2", (15, 512, 16)), -64.0, A.max)
        ts(B("we"), B("wi"), 31, AND)
        cp(B("ewb"), B("we"))
        num = B("b6", (80, 96))
        for m in range(16):
            for s in range(2):
                mm(num, B("lm", m), B("ns", (256 * s + m, 256 * s + 256, 16)), m == 0 and s == 0, False)
        mm(num, B("id14"), B("h"), False, True)
        for m in range(16):
            mm(B("b7", (m, 512, 16)), B("bm", m), B("ewb"), True, True)
        vp = B("b5", (0, 256))
        for s in range(2):
            mm(vp, B("bo"), B("ns", (256 * s, 256 * s + 256)), s == 0, False)
        for m in range(16):
            mm(B("b5", (m, 256, 16)), B("bm", m), B("pl"), False, m == 15)
        cp(B("numu"), num)
        ac(B("numc"), num, AF.Identity, bias=-44.5, scale=1.0 / 32)
        ac(B("numf"), num, AF.Copy)
        gat_tt(B("sh"), B("x", (0, TRX)), B("numu"), B("q"), A.add)
        ts(B("rn"), B("sh"), 1, SHR)
        arrived(pkr, "rq%d" % t, came_from(guest), core)
        ts(B("qi"), B(pkr), 255, AND)
        cp(B("qb"), B("qi"))
        for i in range(5, 16):
            ac(B("qg", (i, 1024, 16)), B("qb"), AF.Copy)
        ts(B("u2i"), B(pkr), 8, SHR)
        tt(B("um"), B("u2i"), B("dm", (0, 64)), A.mult)
        scan(B("us"), B("resa", (0, 64)), B("um"), A.mult, A.add)
        cp(B("u2u"), B("us", (15, 64, 16)))
        gat(B("lig"), B("pt", (0, V)), B("u2u"))
        for i in range(5):
            cp(B("qg", (i, 1024, 16)), B("qb"))
        for hf in range(2):
            gat_tt(B("dg", (16 + 512 * hf, 528 + 512 * hf)), xwin, B("lig", (32 * hf, 32 * hf + 32)), B("qg", (512 * hf, 512 * hf + 512)), A.subtract)
            ac(B("adg", (2 * hf, 2 * hf + 2)), B("dg", (16 + 512 * hf, 528 + 512 * hf)), AF.Abs, scale=64.0)
        gk = B("b1", (0, 64))
        mm(gk, B("id"), B("pcg"), True, False)
        for m in range(16):
            mm(gk, B("lm", m), B("adg", (0, 4), m), False, m == 15)
        ts(B("b3"), B("b7"), B("widx"), A.is_equal)
        for s in range(2):
            tt(B("dv", (256 * s, 256 * s + 256)), vp, B("lic", (256 * s, 256 * s + 256)), A.subtract)
        tt(B("wd"), B("b3"), B("dv"), A.mult)
        tt(B("nrb"), vp, B("trib"), A.add)
        scan(B("sg2"), B("resn", (0, 64)), gk, A.max, A.min)
        ts(B("gkc"), B("sg2", (15, 64, 16)), B("th2k"), A.min)
        ts(B("gpos"), B("gkc"), 2047, AND)
        cp(B("posu"), B("gpos"))
        gat_tt(B(rs), B("dg"), B("posu"), B("qb"), A.add)
        send(guest, rs, "rp%d" % t, (rr, 64))
        for m in range(16):
            mm(B("b4", (0, 16), (2 * m, 2 * m + 2)), B("bm", m), B("moh"), True, True)
        mm(B("b7"), B("id"), B("lic"), True, False)
        mm(B("b7"), B("idf"), B("wd"), False, True)
        if not end:
            ac(B("m256"), B("b4"), AF.Copy, scale=256.0)
        else:
            ac(B("ym2"), B("b4"), AF.Copy)
            dma("y", T.ym[:], T.z_ym2[0:128:16, :], (B("ym2"),), ())
        ac(B("nl"), B("b7"), AF.Identity, bias=1408.0, scale=32.0)
        gat_tt(B("e"), B("numc"), B("expl"), B("nrb"), A.is_equal)
        scan(B("cnt"), B("resa"), B("e"), A.mult, A.add)
        ts(B("l0"), B("cnt", (15, 256, 16)), 0.5, A.is_ge)
        tt(B("l0"), B("l0"), B("un"), A.max)
        tt(B("lt"), B("l0"), B("trx"), A.mult)
        tt(B("xo"), B("lt"), B("numf"), A.max)
        cp(B("xoff", (0, 32, 2)), B("xo"))
        for n in range(15, -1, -1):
            scat(B("x"), B("xoff", (2 * n, 2 * n + 1)), B("rn", (16 * n, 16 * n + 16)))
        if end:
            dma("y", T.yx[:, 0:H + 2 * CAP], B("x", (PAD, PAD + H + 2 * CAP))[0], (B("x", (PAD, PAD + H + 2 * CAP)),), ())
        arrived(rr, "rp%d" % t, came_from(host_of), core)
        tt(B("rz"), B(rr), B("cap"), A.min)
        ts(B("fw", (0, 64)), B("rz"), 0.0, A.is_ge, 1.0 / 512, A.mult)
        agat(B("c"), B("fw"), B("offu"))
        ts(B("gw", (0, 64)), B("rz"), 0.0, A.max)
        gcol = B("x", (PAD + H + CAP * t, PAD + H + CAP * t + CAP))
        came = B("b6", (96, 112))
        for m in range(16):
            mm(came, B("lm", m), B("c", (m, 256, 16)), m == 0, m == 15)
        if not end:
            gat_tt(B("s1"), B("gw"), B("offu"), B("sh"), A.add)
            ts(B("s2"), B("s1"), 255, AND)
            cp(B("q"), B("s2"))
            parity(False)
            qrep_s()
            qrep_v(0, 16 - QA)
        ac(gcol, B("gw", (0, 64)), AF.Copy)
        tt(B("got"), B("h"), came, A.max)
        if not end:
            mm(par, B("sg"), B("got"), False, True)
        tt(B("pz", (0, 16)), B("got"), B("du", (0, 16)), A.mult)
        tt(B("pz", (16, 32)), came, B("du", (16, 32)), A.mult)
        tt(B("po"), B("pz"), B("trp"), A.add)
        cp(B("poff"), B("po"))
        scat(B("pt"), B("poff", (16, 32)), B("nl", (256, 512)))
        scat(B("pt"), B("poff", (0, 16)), B("nl", (0, 256)))
    dma("y", T.yx[:, H + 2 * CAP:W], B("x", (PAD + H + 2 * CAP, TRX))[0], (B("x", (PAD + H + 2 * CAP, TRX)),), ())
    dma("s", T.yp[:], B("pt", (0, V))[0], (B("pt", (0, V)),), ())
    for s, v in total.items():
        g.wait_ge(T.sem[s], v)
